import numpy as np
import ml_dtypes


def mxq(x, axis, fmt="e4m3"):
    dtype, down = {"e4m3": (ml_dtypes.float8_e4m3fn, 7), "e5m2": (ml_dtypes.float8_e5m2, 14)}[fmt]
    v = np.moveaxis(np.asarray(x, np.float32).astype(ml_dtypes.bfloat16).astype(np.float64), axis, -1)
    blocks = v.reshape(v.shape[:-1] + (-1, 32))
    amax = np.abs(blocks).max(-1, keepdims=True)
    byte = np.maximum(np.where(amax > 0, np.frexp(amax)[1] - 1 + 127, 0) - down, 1)
    scale = np.exp2(byte - 127.0)
    codes = (blocks / scale).astype(np.float32).astype(dtype).astype(np.float64)
    return np.moveaxis((codes * scale).reshape(v.shape), -1, axis)


WIDE = False


def mx_kscale(k, group=512):
    if not WIDE:
        return np.ones(k)
    levels = np.array([18, -18])
    if group != 512:
        return np.exp2(np.random.permutation(np.resize(levels, k // group))).repeat(group)
    if k % 512:
        return np.exp2(np.random.permutation(np.resize(levels, k // 32))).repeat(32)
    a = np.empty((k // 512, 16))
    for p in range(k // 512):
        a[p, :8] = np.random.permutation(np.resize(levels, 8))
        for g in range(8):
            far = levels[np.abs(levels - a[p, g]) >= 10]
            a[p, g + 8] = far[np.random.randint(len(far))]
    return np.exp2(a.ravel()).repeat(32)


def f64(x):
    return np.asarray(x).astype(np.float64)


def gelu(v):
    return 0.5 * v * (1.0 + np.tanh(0.7978845608028654 * (v + 0.044715 * v ** 3)))


G, D, M, N = 8, 128, 128, 512


def setup_inputs():
    n = np.random.standard_normal
    s = mx_kscale(D, 0)[:, None]
    return {
        "x": (n((G, D, N)) * s).astype(np.float32),
        "w": (n((G, D, M)) / np.sqrt(D) / s).astype(np.float32),
        "b": (0.5 * n((G, M, 1))).astype(np.float32),
    }


def reference(x, w, b):
    xq = mxq(f64(x), 1, "e4m3")
    y = mxq(f64(w), 1, "e4m3").transpose(0, 2, 1) @ xq
    y = y + f64(b)
    y = gelu(y)
    return y

@@ -1,0 +1,146 @@
+from contextlib import ExitStack
+
+import concourse.mybir as mybir
+
+G, D, M, N = 8, 128, 128, 512
+FLOPS = 2 * G * D * M * N
+
+F32 = mybir.dt.float32
+BF16 = mybir.dt.bfloat16
+U32 = mybir.dt.uint32
+U8 = mybir.dt.uint8
+FP8X4 = mybir.dt.float8_e4m3fn_x4
+GELU = mybir.ActivationFunctionType.Gelu_apprx_tanh
+
+P = 128
+PACK = 4
+ROWS = D // PACK
+SIDE = P // ROWS
+SETS = G // SIDE
+NMM = 128
+LOADS = [("w",0,0,128),("x",0,0,256),("x",0,256,512),("w",1,0,128),("x",1,0,256),("x",1,256,512)]
+PIECES = [(0,0,256),(0,256,512),(1,0,256),(1,256,512)]
+STORES = [(0,0,2,0,512,0),(0,2,4,0,512,0),(1,0,4,0,256,0),(1,0,2,256,512,0),(1,2,4,256,512,0)]
+VORDER = [("c","w",0,0,128),("t",),("q","w",0,0,128),("c","x",0,0,256),("q","x",0,0,256),("f",0),("c","x",0,256,512),("c","w",1,0,128),("q","x",0,256,512),("f",1),("q","w",1,0,128),("c","x",1,0,256),("q","x",1,0,256),("f",2),("c","x",1,256,512),("q","x",1,256,512),("f",3)]
+
+
+def interleave(nc, dst, src):
+    nc.vector.tensor_copy(
+        out=dst.rearrange("p (c i) t -> p c t i", i=4),
+        in_=src.rearrange("p t (c i) -> p c t i", i=4),
+    )
+
+
+def tile_rows_glin_gelu_bias_kernel(tc, x, w, b, out):
+    nc = tc.nc
+    x_rows = x.rearrange("g d n -> (g d) n")
+    w_rows = w.rearrange("g d m -> (g d) m")
+    with ExitStack() as ctx:
+        sb = ctx.enter_context(tc.tile_pool(name="sb", bufs=1))
+        ps = ctx.enter_context(tc.psum_pool(name="ps", bufs=1))
+        ctx.enter_context(tc.manual_schedule())
+
+        b_rows = sb.tile([P, G * ROWS], F32, name="b_rows", align_bytes=64)
+        b_cols = sb.tile([P, G * ROWS], F32, name="b_cols", align_bytes=64)
+        nc.vector.memset(b_rows[:], 0.0)
+        nc.scalar.dma_start(
+            out=b_rows[0:P:ROWS, :].rearrange("q (g i) -> q g i", g=G),
+            in_=b.rearrange("g (q i) o -> q g (i o)", q=SIDE),
+        )
+
+        raw = {}
+        for kind, s, c0, c1 in LOADS:
+            src = x_rows if kind == "x" else w_rows
+            t = sb.tile([P, PACK, c1 - c0], F32, name="raw_%s_%d_%d" % (kind, s, c0), align_bytes=64)
+            rows = src[s * P * PACK : (s + 1) * P * PACK, c0:c1]
+            nc.sync.dma_start(out=t[:], in_=rows.rearrange("(p j) n -> p j n", j=PACK))
+            raw[(kind, s, c0, c1)] = t
+
+        banks = []
+        for k in range(2 * SIDE):
+            bank = ps.tile([M, 512], F32, name="bank_%d" % k)
+            banks.append(bank)
+
+        res = {}
+        for s, g0, g1, c0, c1, q in STORES:
+            t = sb.tile([M, g1 - g0, c1 - c0], F32, name="res_%d_%d_%d" % (s, g0, c0), align_bytes=64)
+            res[(s, g0, g1, c0, c1, q)] = t
+
+        grouped = {}
+        codes = {}
+        scales = {}
+        done = set()
+        stored = set()
+
+        def copy(kind, s, c0, c1):
+            for key in raw:
+                if key[0] == kind and key[1] == s and key[2] <= c0 and c1 <= key[3]:
+                    t = sb.tile([P, c1 - c0, PACK], BF16, name="grp_%s_%d_%d" % (kind, s, c0), align_bytes=64)
+                    interleave(nc, t[:], raw[key][:, :, c0 - key[2] : c1 - key[2]])
+                    grouped[(kind, s, c0)] = t
+
+        def quant(kind, s, c0, c1):
+            cd = sb.tile([P, c1 - c0], U32, name="codes_%s_%d_%d" % (kind, s, c0), align_bytes=64)
+            sc = sb.tile([P, c1 - c0], U8, name="scales_%s_%d_%d" % (kind, s, c0), align_bytes=64)
+            nc.vector.quantize_mx(
+                out=cd[:].bitcast(FP8X4),
+                scales=sc[:],
+                in_=grouped[(kind, s, c0)][:].rearrange("p n t -> p (n t)"),
+            )
+            codes[(kind, s, c0, c1)] = cd
+            scales[(kind, s, c0, c1)] = sc
+
+        def finish(index):
+            s, c0, c1 = PIECES[index]
+            wc = codes[("w", s, 0, M)]
+            ws = scales[("w", s, 0, M)]
+            for c in range(SIDE):
+                rows = slice(c * ROWS, (c + 1) * ROWS)
+                bank = banks[2 * c + index % 2]
+                for n0 in range(c0, c1, NMM):
+                    for key in codes:
+                        if key[0] == "x" and key[1] == s and key[2] <= n0 and n0 + NMM <= key[3]:
+                            cols = slice(n0 - key[2], n0 - key[2] + NMM)
+                            nc.tensor.matmul_mx(
+                                out=bank[:, n0 - c0 : n0 - c0 + NMM],
+                                lhsT=wc[rows, :].bitcast(FP8X4),
+                                lhsT_scale=ws[rows, :],
+                                rhs=codes[key][rows, cols].bitcast(FP8X4),
+                                rhs_scale=scales[key][rows, cols],
+                                start=True,
+                                stop=True,
+                            )
+            for c in range(SIDE):
+                bank = banks[2 * c + index % 2]
+                g = s * SIDE + c
+                for key in res:
+                    if key[0] == s and key[1] <= c < key[2]:
+                        lo = max(c0, key[3])
+                        hi = min(c1, key[4])
+                        if lo < hi:
+                            nc.scalar.activation(
+                                out=res[key][:, c - key[1], lo - key[3] : hi - key[3]],
+                                in_=bank[:, lo - c0 : hi - c0],
+                                func=GELU,
+                                bias=b_cols[:, g * ROWS : g * ROWS + 1],
+                            )
+                            for n in range(lo, hi, 64):
+                                done.add((s, c, n))
+                for key in res:
+                    if key not in stored and all(
+                        (key[0], cc, n) in done for cc in range(key[1], key[2]) for n in range(key[3], key[4], 64)
+                    ):
+                        stored.add(key)
+                        dst = out[key[0] * SIDE + key[1] : key[0] * SIDE + key[2], :, key[3] : key[4]]
+                        eng = nc.sync if key[5] == 0 else nc.scalar
+                        eng.dma_start(out=dst.rearrange("g m n -> m g n"), in_=res[key][:])
+
+        for step in VORDER:
+            if step[0] == "t":
+                nc.vector.transpose(b_cols[:], b_rows[:])
+            elif step[0] == "c":
+                copy(step[1], step[2], step[3], step[4])
+            elif step[0] == "q":
+                quant(step[1], step[2], step[3], step[4])
+            else:
+                finish(step[1])

@@ -20,7 +20,7 @@ SETS = G // SIDE
 NMM = 128
 LOADS = [("w",0,0,128),("x",0,0,256),("x",0,256,512),("w",1,0,128),("x",1,0,256),("x",1,256,512)]
 PIECES = [(0,0,256),(0,256,512),(1,0,256),(1,256,512)]
-STORES = [(0,0,2,0,512,0),(0,2,4,0,512,0),(1,0,4,0,256,0),(1,0,2,256,512,0),(1,2,4,256,512,0)]
+STORES = [(0,0,2,0,256,0),(0,2,4,0,256,0),(0,0,2,256,512,0),(0,2,4,256,512,0),(1,0,2,0,256,0),(1,2,4,0,256,0),(1,0,2,256,512,0),(1,2,4,256,512,0)]
 VORDER = [("c","w",0,0,128),("t",),("q","w",0,0,128),("c","x",0,0,256),("q","x",0,0,256),("f",0),("c","x",0,256,512),("c","w",1,0,128),("q","x",0,256,512),("f",1),("q","w",1,0,128),("c","x",1,0,256),("q","x",1,0,256),("f",2),("c","x",1,256,512),("q","x",1,256,512),("f",3)]
 
 
@@ -43,10 +43,6 @@ def tile_rows_glin_gelu_bias_kernel(tc, x, w, b, out):
         b_rows = sb.tile([P, G * ROWS], F32, name="b_rows", align_bytes=64)
         b_cols = sb.tile([P, G * ROWS], F32, name="b_cols", align_bytes=64)
         nc.vector.memset(b_rows[:], 0.0)
-        nc.scalar.dma_start(
-            out=b_rows[0:P:ROWS, :].rearrange("q (g i) -> q g i", g=G),
-            in_=b.rearrange("g (q i) o -> q g (i o)", q=SIDE),
-        )
 
         raw = {}
         for kind, s, c0, c1 in LOADS:
@@ -55,6 +51,11 @@ def tile_rows_glin_gelu_bias_kernel(tc, x, w, b, out):
             rows = src[s * P * PACK : (s + 1) * P * PACK, c0:c1]
             nc.sync.dma_start(out=t[:], in_=rows.rearrange("(p j) n -> p j n", j=PACK))
             raw[(kind, s, c0, c1)] = t
+            if len(raw) == 1:
+                nc.sync.dma_start(
+                    out=b_rows[0:P:ROWS, :].rearrange("q (g i) -> q g i", g=G),
+                    in_=b.rearrange("g (q i) o -> q g (i o)", q=SIDE),
+                )
 
         banks = []
         for k in range(2 * SIDE):

@@ -18,10 +18,10 @@ ROWS = D // PACK
 SIDE = P // ROWS
 SETS = G // SIDE
 NMM = 128
-LOADS = [("w",0,0,128),("x",0,0,256),("x",0,256,512),("w",1,0,128),("x",1,0,256),("x",1,256,512)]
+LOADS = [("w",0,0,128),("x",0,0,512),("x",1,0,512),("w",1,0,128)]
 PIECES = [(0,0,256),(0,256,512),(1,0,256),(1,256,512)]
 STORES = [(0,0,2,0,256,0),(0,2,4,0,256,0),(0,0,2,256,512,0),(0,2,4,256,512,0),(1,0,2,0,256,0),(1,2,4,0,256,0),(1,0,2,256,512,0),(1,2,4,256,512,0)]
-VORDER = [("c","w",0,0,128),("t",),("q","w",0,0,128),("c","x",0,0,256),("q","x",0,0,256),("f",0),("c","x",0,256,512),("c","w",1,0,128),("q","x",0,256,512),("f",1),("q","w",1,0,128),("c","x",1,0,256),("q","x",1,0,256),("f",2),("c","x",1,256,512),("q","x",1,256,512),("f",3)]
+VORDER = [("c","w",0,0,128),("q","w",0,0,128),("c","x",0,0,256),("t",),("q","x",0,0,256),("f",0),("c","x",0,256,512),("q","x",0,256,512),("f",1),("c","x",1,0,256),("c","w",1,0,128),("q","x",1,0,256),("q","w",1,0,128),("f",2),("c","x",1,256,512),("q","x",1,256,512),("f",3)]
 
 
 def interleave(nc, dst, src):
@@ -51,7 +51,7 @@ def tile_rows_glin_gelu_bias_kernel(tc, x, w, b, out):
             rows = src[s * P * PACK : (s + 1) * P * PACK, c0:c1]
             nc.sync.dma_start(out=t[:], in_=rows.rearrange("(p j) n -> p j n", j=PACK))
             raw[(kind, s, c0, c1)] = t
-            if len(raw) == 1:
+            if len(raw) == 2:
                 nc.sync.dma_start(
                     out=b_rows[0:P:ROWS, :].rearrange("q (g i) -> q g i", g=G),
                     in_=b.rearrange("g (q i) o -> q g (i o)", q=SIDE),

@@ -18,10 +18,10 @@ ROWS = D // PACK
 SIDE = P // ROWS
 SETS = G // SIDE
 NMM = 128
-LOADS = [("w",0,0,128),("x",0,0,512),("x",1,0,512),("w",1,0,128)]
+LOADS = [("w",0,0,128),("x",0,0,256),("x",0,256,512),("x",1,0,256),("w",1,0,128),("x",1,256,512)]
 PIECES = [(0,0,256),(0,256,512),(1,0,256),(1,256,512)]
 STORES = [(0,0,2,0,256,0),(0,2,4,0,256,0),(0,0,2,256,512,0),(0,2,4,256,512,0),(1,0,2,0,256,0),(1,2,4,0,256,0),(1,0,2,256,512,0),(1,2,4,256,512,0)]
-VORDER = [("c","w",0,0,128),("q","w",0,0,128),("c","x",0,0,256),("t",),("q","x",0,0,256),("f",0),("c","x",0,256,512),("q","x",0,256,512),("f",1),("c","x",1,0,256),("c","w",1,0,128),("q","x",1,0,256),("q","w",1,0,128),("f",2),("c","x",1,256,512),("q","x",1,256,512),("f",3)]
+VORDER = [("c","w",0,0,128),("t",),("q","w",0,0,128),("c","x",0,0,128),("c","x",0,128,256),("q","x",0,0,128),("q","x",0,128,256),("f",0),("c","x",0,256,384),("c","x",0,384,512),("q","x",0,256,384),("q","x",0,384,512),("f",1),("c","x",1,0,256),("c","w",1,0,128),("q","x",1,0,256),("q","w",1,0,128),("f",2),("c","x",1,256,384),("c","x",1,384,512),("q","x",1,256,384),("q","x",1,384,512),("f",3)]
 
 
 def interleave(nc, dst, src):
@@ -51,7 +51,7 @@ def tile_rows_glin_gelu_bias_kernel(tc, x, w, b, out):
             rows = src[s * P * PACK : (s + 1) * P * PACK, c0:c1]
             nc.sync.dma_start(out=t[:], in_=rows.rearrange("(p j) n -> p j n", j=PACK))
             raw[(kind, s, c0, c1)] = t
-            if len(raw) == 2:
+            if len(raw) == 1:
                 nc.sync.dma_start(
                     out=b_rows[0:P:ROWS, :].rearrange("q (g i) -> q g i", g=G),
                     in_=b.rearrange("g (q i) o -> q g (i o)", q=SIDE),

from contextlib import ExitStack

import concourse.mybir as mybir

G, D, M, N = 8, 128, 128, 512
FLOPS = 2 * G * D * M * N

F32 = mybir.dt.float32
BF16 = mybir.dt.bfloat16
U32 = mybir.dt.uint32
U8 = mybir.dt.uint8
FP8X4 = mybir.dt.float8_e4m3fn_x4
GELU = mybir.ActivationFunctionType.Gelu_apprx_tanh

P = 128
PACK = 4
ROWS = D // PACK
SIDE = P // ROWS
SETS = G // SIDE
NMM = 128
LOADS = [("w",0,0,128),("x",0,0,256),("x",0,256,512),("x",1,0,256),("w",1,0,128),("x",1,256,512)]
PIECES = [(0,0,256),(0,256,512),(1,0,256),(1,256,512)]
STORES = [(0,0,2,0,256,0),(0,2,4,0,256,0),(0,0,2,256,512,0),(0,2,4,256,512,0),(1,0,2,0,256,0),(1,2,4,0,256,0),(1,0,2,256,512,0),(1,2,4,256,512,0)]
VORDER = [("c","w",0,0,128),("t",),("q","w",0,0,128),("c","x",0,0,128),("c","x",0,128,256),("q","x",0,0,128),("q","x",0,128,256),("f",0),("c","x",0,256,384),("c","x",0,384,512),("q","x",0,256,384),("q","x",0,384,512),("f",1),("c","x",1,0,256),("c","w",1,0,128),("q","x",1,0,256),("q","w",1,0,128),("f",2),("c","x",1,256,384),("c","x",1,384,512),("q","x",1,256,384),("q","x",1,384,512),("f",3)]


def interleave(nc, dst, src):
    nc.vector.tensor_copy(
        out=dst.rearrange("p (c i) t -> p c t i", i=4),
        in_=src.rearrange("p t (c i) -> p c t i", i=4),
    )


def tile_rows_glin_gelu_bias_kernel(tc, x, w, b, out):
    nc = tc.nc
    x_rows = x.rearrange("g d n -> (g d) n")
    w_rows = w.rearrange("g d m -> (g d) m")
    with ExitStack() as ctx:
        sb = ctx.enter_context(tc.tile_pool(name="sb", bufs=1))
        ps = ctx.enter_context(tc.psum_pool(name="ps", bufs=1))
        ctx.enter_context(tc.manual_schedule())

        b_rows = sb.tile([P, G * ROWS], F32, name="b_rows", align_bytes=64)
        b_cols = sb.tile([P, G * ROWS], F32, name="b_cols", align_bytes=64)
        nc.vector.memset(b_rows[:], 0.0)

        raw = {}
        for kind, s, c0, c1 in LOADS:
            src = x_rows if kind == "x" else w_rows
            t = sb.tile([P, PACK, c1 - c0], F32, name="raw_%s_%d_%d" % (kind, s, c0), align_bytes=64)
            rows = src[s * P * PACK : (s + 1) * P * PACK, c0:c1]
            nc.sync.dma_start(out=t[:], in_=rows.rearrange("(p j) n -> p j n", j=PACK))
            raw[(kind, s, c0, c1)] = t
            if len(raw) == 1:
                nc.sync.dma_start(
                    out=b_rows[0:P:ROWS, :].rearrange("q (g i) -> q g i", g=G),
                    in_=b.rearrange("g (q i) o -> q g (i o)", q=SIDE),
                )

        banks = []
        for k in range(2 * SIDE):
            bank = ps.tile([M, 512], F32, name="bank_%d" % k)
            banks.append(bank)

        res = {}
        for s, g0, g1, c0, c1, q in STORES:
            t = sb.tile([M, g1 - g0, c1 - c0], F32, name="res_%d_%d_%d" % (s, g0, c0), align_bytes=64)
            res[(s, g0, g1, c0, c1, q)] = t

        grouped = {}
        codes = {}
        scales = {}
        done = set()
        stored = set()

        def copy(kind, s, c0, c1):
            for key in raw:
                if key[0] == kind and key[1] == s and key[2] <= c0 and c1 <= key[3]:
                    t = sb.tile([P, c1 - c0, PACK], BF16, name="grp_%s_%d_%d" % (kind, s, c0), align_bytes=64)
                    interleave(nc, t[:], raw[key][:, :, c0 - key[2] : c1 - key[2]])
                    grouped[(kind, s, c0)] = t

        def quant(kind, s, c0, c1):
            cd = sb.tile([P, c1 - c0], U32, name="codes_%s_%d_%d" % (kind, s, c0), align_bytes=64)
            sc = sb.tile([P, c1 - c0], U8, name="scales_%s_%d_%d" % (kind, s, c0), align_bytes=64)
            nc.vector.quantize_mx(
                out=cd[:].bitcast(FP8X4),
                scales=sc[:],
                in_=grouped[(kind, s, c0)][:].rearrange("p n t -> p (n t)"),
            )
            codes[(kind, s, c0, c1)] = cd
            scales[(kind, s, c0, c1)] = sc

        def finish(index):
            s, c0, c1 = PIECES[index]
            wc = codes[("w", s, 0, M)]
            ws = scales[("w", s, 0, M)]
            for c in range(SIDE):
                rows = slice(c * ROWS, (c + 1) * ROWS)
                bank = banks[2 * c + index % 2]
                for n0 in range(c0, c1, NMM):
                    for key in codes:
                        if key[0] == "x" and key[1] == s and key[2] <= n0 and n0 + NMM <= key[3]:
                            cols = slice(n0 - key[2], n0 - key[2] + NMM)
                            nc.tensor.matmul_mx(
                                out=bank[:, n0 - c0 : n0 - c0 + NMM],
                                lhsT=wc[rows, :].bitcast(FP8X4),
                                lhsT_scale=ws[rows, :],
                                rhs=codes[key][rows, cols].bitcast(FP8X4),
                                rhs_scale=scales[key][rows, cols],
                                start=True,
                                stop=True,
                            )
            for c in range(SIDE):
                bank = banks[2 * c + index % 2]
                g = s * SIDE + c
                for key in res:
                    if key[0] == s and key[1] <= c < key[2]:
                        lo = max(c0, key[3])
                        hi = min(c1, key[4])
                        if lo < hi:
                            nc.scalar.activation(
                                out=res[key][:, c - key[1], lo - key[3] : hi - key[3]],
                                in_=bank[:, lo - c0 : hi - c0],
                                func=GELU,
                                bias=b_cols[:, g * ROWS : g * ROWS + 1],
                            )
                            for n in range(lo, hi, 64):
                                done.add((s, c, n))
                for key in res:
                    if key not in stored and all(
                        (key[0], cc, n) in done for cc in range(key[1], key[2]) for n in range(key[3], key[4], 64)
                    ):
                        stored.add(key)
                        dst = out[key[0] * SIDE + key[1] : key[0] * SIDE + key[2], :, key[3] : key[4]]
                        eng = nc.sync if key[5] == 0 else nc.scalar
                        eng.dma_start(out=dst.rearrange("g m n -> m g n"), in_=res[key][:])

        for step in VORDER:
            if step[0] == "t":
                nc.vector.transpose(b_cols[:], b_rows[:])
            elif step[0] == "c":
                copy(step[1], step[2], step[3], step[4])
            elif step[0] == "q":
                quant(step[1], step[2], step[3], step[4])
            else:
                finish(step[1])
